import numpy as np
import ml_dtypes


def mxq(x, axis, fmt="e4m3"):
    dtype, down = {"e4m3": (ml_dtypes.float8_e4m3fn, 7), "e5m2": (ml_dtypes.float8_e5m2, 14)}[fmt]
    v = np.moveaxis(np.asarray(x, np.float32).astype(ml_dtypes.bfloat16).astype(np.float64), axis, -1)
    blocks = v.reshape(v.shape[:-1] + (-1, 32))
    amax = np.abs(blocks).max(-1, keepdims=True)
    byte = np.maximum(np.where(amax > 0, np.frexp(amax)[1] - 1 + 127, 0) - down, 1)
    scale = np.exp2(byte - 127.0)
    codes = (blocks / scale).astype(np.float32).astype(dtype).astype(np.float64)
    return np.moveaxis((codes * scale).reshape(v.shape), -1, axis)


WIDE = False


def mx_kscale(k):
    if not WIDE:
        return np.ones(k)
    levels = np.array([10, -10, 5, -5, 0])
    if k % 512:
        return np.exp2(np.random.permutation(np.resize(levels, k // 32))).repeat(32)
    a = np.empty((k // 512, 16))
    for p in range(k // 512):
        a[p, :8] = np.random.permutation(np.resize(levels, 8))
        for g in range(8):
            far = levels[np.abs(levels - a[p, g]) >= 10]
            a[p, g + 8] = far[np.random.randint(len(far))]
    return np.exp2(a.ravel()).repeat(32)


def f64(x):
    return np.asarray(x).astype(np.float64)


def striped(idx):
    return np.tile(np.asarray(idx).reshape(-1, 16).T, (8, 1)).astype(np.uint16)


def unstriped(offs):
    return offs[:16].T.reshape(-1).astype(np.int64)


def striped8(idx):
    return np.asarray(idx).reshape(8, -1, 16).transpose(0, 2, 1).reshape(128, -1).astype(np.uint16)


def unstriped8(offs):
    return offs.reshape(8, 16, -1).transpose(0, 2, 1).reshape(8, -1).astype(np.int64)


def pick8(x, idx, run):
    r = np.arange(len(x))
    return x[r[:, None], idx[r % (8 * run) // run]]


E2M1 = np.array([0.0, 0.5, 1.0, 1.5, 2.0, 3.0, 4.0, 6.0, -0.0, -0.5, -1.0, -1.5, -2.0, -3.0, -4.0, -6.0])


def pack_weight(w, fmt):
    k, n = w.shape
    w = f64(np.asarray(w, np.float32).astype(ml_dtypes.bfloat16)).reshape(k // 32, 32, n)
    amax = np.abs(w).max(1)
    if fmt == "e4m3":
        byte = np.frexp(amax)[1] - 1 + 127 - 7
    else:
        mant, ex = np.frexp(amax / 6.0)
        byte = np.where(mant > 0.5, ex, ex - 1) + 127
    byte = np.clip(np.where(amax > 0, byte, 1), 1, 254)
    scaled = (w * np.exp2(127.0 - byte)[:, None, :]).reshape(k, n).astype(np.float32)
    by_word = np.ascontiguousarray(scaled.reshape(k // 512, 128, 4, n).transpose(0, 1, 3, 2))
    if fmt == "e4m3":
        words = by_word.astype(ml_dtypes.float8_e4m3fn).view(np.uint8)
    else:
        c = by_word.astype(ml_dtypes.float4_e2m1fn).view(np.uint8) & 0xF
        words = (c[..., 0::2] | (c[..., 1::2] << 4)).reshape(k // 512, 128, 2 * n)
    return np.ascontiguousarray(words), np.ascontiguousarray(byte.astype(np.uint8).reshape(k // 512, 16, n))


def unpack_weight(words, scales, fmt):
    g, _, n = scales.shape
    words = np.ascontiguousarray(words).reshape(g, 128, n, -1)
    if fmt == "e4m3":
        vals = words.view(ml_dtypes.float8_e4m3fn).astype(np.float64)
    else:
        nib = np.empty((g, 128, n, 4), np.uint8)
        nib[..., 0::2] = words & 0xF
        nib[..., 1::2] = words >> 4
        vals = E2M1[nib]
    vals = vals * np.repeat(np.exp2(scales.astype(np.float64) - 127.0), 8, axis=1)[..., None]
    return vals.transpose(0, 1, 3, 2).reshape(g * 512, n)


K, J, R, T, F, Z, M, O, C, N = 512, 256, 512, 1024, 1024, 512, 1024, 128, 512, 256


def setup_inputs():
    n = np.random.standard_normal
    idx = np.random.permutation(T)[:J]
    idx2 = np.stack([np.random.permutation(F)[:R] for _ in range(8)])
    idx3 = np.stack([np.random.permutation(F)[:R] for _ in range(8)])
    idx4 = np.random.permutation(M)[:J]
    idx5 = np.stack([np.random.permutation(C)[:J] for _ in range(8)])
    idx6 = np.stack([np.random.permutation(C)[:J] for _ in range(8)])
    idx7 = np.stack([np.random.permutation(J)[:O] for _ in range(8)])
    fk = mx_kscale(K)
    fz = mx_kscale(Z)
    fr = mx_kscale(R)
    xtp = pack_weight(n((K, T)) * fk[:, None], "e2m1")
    xop = pack_weight(n((Z, M)) / fz[:, None], "e2m1")
    w2p = pack_weight(n((Z, R)) * 1 / np.sqrt(Z) * fz[:, None], "e4m3")
    wbp = pack_weight(n((R, N)) * 1 / np.sqrt(R) / fr[:, None], "e4m3")
    return {
        "xt_words": xtp[0],
        "xt_scales": xtp[1],
        "ua": (np.random.randint(-7, 8, (K, F)).astype(np.float64)).astype(np.float32),
        "ha": ((np.random.randint(8, 19, (K, 1)) / 1024.0) / fk[:, None]).astype(np.float32),
        "hb": ((np.random.randint(8, 19, (K, 1)) / 1024.0) / fk[:, None]).astype(np.float32),
        "xo_words": xop[0],
        "xo_scales": xop[1],
        "w2_words": w2p[0],
        "w2_scales": w2p[1],
        "sa": (np.random.uniform(0.5, 1.6, (R, 1))).astype(np.float32),
        "sb": (np.random.uniform(0.5, 1.6, (R, 1)) * fr[:, None]).astype(np.float32),
        "wb_words": wbp[0],
        "wb_scales": wbp[1],
        "offs": striped(idx),
        "offs2": striped8(idx2),
        "offs3": striped8(idx3),
        "offs4": striped(idx4),
        "offs5": striped8(idx5),
        "offs6": striped8(idx6),
        "offs7": striped8(idx7),
    }


def reference(xt_words, xt_scales, ua, ha, hb, xo_words, xo_scales, w2_words, w2_scales, sa, sb, wb_words, wb_scales, offs, offs2, offs3, offs4, offs5, offs6, offs7):
    idx = unstriped(offs)
    idx2 = unstriped8(offs2)
    idx3 = unstriped8(offs3)
    idx4 = unstriped(offs4)
    idx5 = unstriped8(offs5)
    idx6 = unstriped8(offs6)
    idx7 = unstriped8(offs7)
    xtu = unpack_weight(xt_words, xt_scales, "e2m1")
    xou = unpack_weight(xo_words, xo_scales, "e2m1")
    w2u = unpack_weight(w2_words, w2_scales, "e4m3")
    wbu = unpack_weight(wb_words, wb_scales, "e4m3")
    wc = pick8(f64(ua), idx2, 64) * f64(ha) - pick8(f64(ua), idx3, 64) * f64(hb)
    wcq = mxq(wc, 0, "e4m3")
    xtidxg = xtu[:, idx]
    a = wcq.T @ xtidxg
    xoidx4g = xou[:, idx4]
    b = w2u.T @ xoidx4g
    pw = np.zeros((R, C))
    pw[np.arange(R)[:, None], idx5[np.arange(R) % 512 // 64]] = a
    g1 = np.maximum(pick8(pw, idx6, 64) * f64(sa), b)
    hid = pick8(g1, idx7, 64) * f64(sb)
    hidq = mxq(hid, 0, "e4m3")
    y = wbu.T @ hidq
    return y

@@ -1,0 +1,224 @@
+from contextlib import ExitStack
+
+import concourse.mybir as mybir
+
+F32 = mybir.dt.float32
+BF16 = mybir.dt.bfloat16
+I32 = mybir.dt.int32
+U16 = mybir.dt.uint16
+U8 = mybir.dt.uint8
+FP8X4 = mybir.dt.float8_e4m3fn_x4
+FP4X4 = mybir.dt.float4_e2m1fn_x4
+COPY = mybir.ActivationFunctionType.Copy
+SUB = mybir.AluOpType.subtract
+MAX = mybir.AluOpType.max
+
+K, J, R, T, F, Z, M, O, C, N = 512, 256, 512, 1024, 1024, 512, 1024, 128, 512, 256
+P = 128
+PACK = 4
+HALF = R // 2
+HM = HALF // PACK
+
+FLOPS = 2 * K * R * J + 2 * Z * R * J + 2 * R * N * O
+
+
+def tile_picked_tokens_codegap_two_answered_one_plain_kernel(
+    tc, xt_words, xt_scales, ua, ha, hb, xo_words, xo_scales, w2_words, w2_scales, sa, sb,
+    wb_words, wb_scales, offs, offs2, offs3, offs4, offs5, offs6, offs7, out,
+):
+    nc = tc.nc
+    with ExitStack() as ctx:
+        pool = ctx.enter_context(tc.tile_pool(name="sbuf", bufs=1))
+        psum = ctx.enter_context(tc.psum_pool(name="psum", bufs=1))
+
+        def sb_tile(shape, dtype, name):
+            return pool.tile(shape, dtype, name=name, align_bytes=64)
+
+        def load_list(src, name):
+            tile = sb_tile(list(src.shape), U16, name)
+            nc.sync.dma_start(tile[:], src)
+            return tile
+
+        def load_rows(src, name):
+            tile = sb_tile([P, PACK], F32, name)
+            nc.sync.dma_start(tile[:], src.rearrange("(p t) o -> p (t o)", t=PACK))
+            return tile
+
+        def zeroed_plane(width, name):
+            tile = sb_tile([P, width], U8, name)
+            nc.vector.memset(tile[:].bitcast(I32), 0)
+            return tile
+
+        def load_plane(tile, src):
+            for q in range(4):
+                nc.sync.dma_start(
+                    tile[32 * q : 32 * q + 4, :].bitcast(I32), src[0, 4 * q : 4 * q + 4, :].bitcast(I32)
+                )
+
+        xt_plane = zeroed_plane(T, "xt_plane")
+        xo_plane = zeroed_plane(M, "xo_plane")
+        w2_plane = zeroed_plane(R, "w2_plane")
+        wb_plane = zeroed_plane(N, "wb_plane")
+        board = []
+        for t in range(PACK):
+            tile = sb_tile([P, C], F32, f"board{t}")
+            nc.vector.memset(tile[:], 0.0)
+            board.append(tile)
+
+        ua_rows = ua.rearrange("(p j) f -> p j f", j=PACK)
+        table = [sb_tile([P, F], F32, f"table{j}") for j in range(PACK)]
+        xt_all = sb_tile([P, T], U16, "xt_all")
+        xo_all = sb_tile([P, M], U16, "xo_all")
+        w2_all = sb_tile([P, R], I32, "w2_all")
+        list2 = load_list(offs2, "list2")
+        nc.scalar.dma_start(table[0][:], ua_rows[:, 0, :])
+        ha_t = load_rows(ha, "ha_t")
+        list3 = load_list(offs3, "list3")
+        hb_t = load_rows(hb, "hb_t")
+        list1 = load_list(offs, "list1")
+        nc.scalar.dma_start(xt_all[:].bitcast(I32), xt_words[0].bitcast(I32))
+        nc.scalar.dma_start(table[1][:], ua_rows[:, 1, :])
+        load_plane(xt_plane, xt_scales)
+        list4 = load_list(offs4, "list4")
+        nc.sync.dma_start(xo_all[:].bitcast(I32), xo_words[0].bitcast(I32))
+        nc.sync.dma_start(table[2][:], ua_rows[:, 2, :])
+        load_plane(xo_plane, xo_scales)
+        nc.sync.dma_start(w2_all[:], w2_words[0].rearrange("p n t -> p (n t)").bitcast(I32))
+        load_plane(w2_plane, w2_scales)
+        nc.sync.dma_start(table[3][:], ua_rows[:, 3, :])
+        list5 = load_list(offs5, "list5")
+        sa_t = load_rows(sa, "sa_t")
+        list6 = load_list(offs6, "list6")
+        list7 = load_list(offs7, "list7")
+        sb_t = load_rows(sb, "sb_t")
+        wb_all = sb_tile([P, N], I32, "wb_all")
+        nc.sync.dma_start(wb_all[:], wb_words[0].rearrange("p n t -> p (n t)").bitcast(I32))
+        load_plane(wb_plane, wb_scales)
+
+        first = [sb_tile([P, R], F32, f"first{j}") for j in range(PACK)]
+        second = [sb_tile([P, R], F32, f"second{j}") for j in range(PACK)]
+        diff = [sb_tile([P, PACK, PACK, HM], BF16, f"diff{h}") for h in range(2)]
+        grouped = [sb_tile([P, PACK, HM, PACK], BF16, f"grouped{h}") for h in range(2)]
+        wc_codes = [sb_tile([P, P], I32, f"wc_codes{t}") for t in range(PACK)]
+        wc_plane = [sb_tile([P, P], U8, f"wc_plane{t}") for t in range(PACK)]
+
+        def fetch(j, lo, hi):
+            for dst, lst, step in ((first, list2, ha_t), (second, list3, hb_t)):
+                nc.scalar.activation(
+                    dst[j][:, lo:hi], table[j][:].indirect(lst[:, lo // 16 : hi // 16]), COPY,
+                    scale=step[:, j : j + 1],
+                )
+
+        def subtract(j, h):
+            cols = slice(h * HALF, (h + 1) * HALF)
+            nc.vector.tensor_tensor(
+                diff[h][:, j, :, :].rearrange("p t m -> p m t"),
+                first[j][:, cols].rearrange("p (m t) -> p m t", t=PACK),
+                second[j][:, cols].rearrange("p (m t) -> p m t", t=PACK),
+                SUB,
+            )
+
+        def weave(h, t0, t1):
+            nc.vector.tensor_copy(
+                grouped[h][:, t0:t1, :, :].rearrange("p t m j -> p (t m) j"),
+                diff[h][:, :, t0:t1, :].rearrange("p j t m -> p (t m) j"),
+            )
+
+        def quantise(h, t):
+            cols = slice(h * HM, (h + 1) * HM)
+            nc.vector.quantize_mx(
+                out=wc_codes[t][:, cols].bitcast(FP8X4),
+                scales=wc_plane[t][:, cols],
+                in_=grouped[h][:, t, :, :].rearrange("p m j -> p (m j)"),
+            )
+
+        def pick(words_all, plane_all, lst, name):
+            words = sb_tile([P, J], U16, name + "_words")
+            plane = sb_tile([P, J], U8, name + "_plane")
+            nc.vector.tensor_copy(words[:], words_all[:].indirect(lst[:]))
+            nc.vector.tensor_copy(plane[:], plane_all[:].indirect(lst[:]))
+            return words, plane
+
+        xt_pick, xt_pick_plane = pick(xt_all, xt_plane, list1, "xt_pick")
+        fetch(0, 0, R)
+        subtract(0, 0)
+        subtract(0, 1)
+        xo_pick, xo_pick_plane = pick(xo_all, xo_plane, list4, "xo_pick")
+        fetch(1, 0, R)
+        subtract(1, 0)
+        subtract(1, 1)
+        w2_dealt = sb_tile([P, PACK, P], I32, "w2_dealt")
+        w2_dealt_plane = sb_tile([P, PACK, P], U8, "w2_dealt_plane")
+        nc.vector.tensor_copy(w2_dealt[:], w2_all[:].rearrange("p (m t) -> p t m", t=PACK))
+        nc.vector.tensor_copy(w2_dealt_plane[:], w2_plane[:].rearrange("p (m t) -> p t m", t=PACK))
+        b_bank = [psum.tile([P, 2, J], F32, name=f"b_bank{u}") for u in range(2)]
+        for t in range(PACK):
+            nc.tensor.matmul_mx(
+                out=b_bank[t // 2][:, t % 2, :],
+                lhsT=w2_dealt[:, t, :].bitcast(FP8X4), lhsT_scale=w2_dealt_plane[:, t, :],
+                rhs=xo_pick[:].bitcast(FP4X4), rhs_scale=xo_pick_plane[:],
+                start=True, stop=True,
+            )
+
+        fetch(2, 0, HALF)
+        subtract(2, 0)
+        fetch(3, 0, HALF)
+        subtract(3, 0)
+        fetch(2, HALF, R)
+        weave(0, 0, PACK)
+        subtract(2, 1)
+        for t in range(PACK):
+            quantise(0, t)
+        fetch(3, HALF, R)
+        subtract(3, 1)
+        weave(1, 0, 1)
+        weave(1, 1, 2)
+        quantise(1, 0)
+        weave(1, 2, 4)
+        for t in range(1, PACK):
+            quantise(1, t)
+
+        hid_rows = sb_tile([P, PACK, O], BF16, "hid_rows")
+        for t in range(PACK):
+            a_bank = psum.tile([P, J], F32, name=f"a_bank{t}")
+            nc.tensor.matmul_mx(
+                out=a_bank[:],
+                lhsT=wc_codes[t][:].bitcast(FP8X4), lhsT_scale=wc_plane[t][:],
+                rhs=xt_pick[:].bitcast(FP4X4), rhs_scale=xt_pick_plane[:],
+                start=True, stop=True,
+            )
+            a_rows = sb_tile([P, J], F32, f"a_rows{t}")
+            nc.scalar.copy(a_rows[:], a_bank[:])
+            nc.vector.tensor_copy(board[t][:].indirect(list5[:]), a_rows[:])
+            read = sb_tile([P, J], F32, f"read{t}")
+            nc.scalar.activation(read[:], board[t][:].indirect(list6[:]), COPY, scale=sa_t[:, t : t + 1])
+            answer = sb_tile([P, J], F32, f"answer{t}")
+            nc.vector.tensor_tensor(answer[:], b_bank[t // 2][:, t % 2, :], read[:], MAX)
+            nc.scalar.activation(
+                hid_rows[:, t, :], answer[:].indirect(list7[:]), COPY, scale=sb_t[:, t : t + 1]
+            )
+
+        hid_grouped = sb_tile([P, O, PACK], BF16, "hid_grouped")
+        nc.vector.tensor_copy(hid_grouped[:], hid_rows[:].rearrange("p t o -> p o t"))
+        hid_codes = sb_tile([P, O], I32, "hid_codes")
+        hid_plane = sb_tile([P, O], U8, "hid_plane")
+        nc.vector.quantize_mx(
+            out=hid_codes[:].bitcast(FP8X4), scales=hid_plane[:],
+            in_=hid_grouped[:].rearrange("p o t -> p (o t)"),
+        )
+        for u in range(2):
+            cols = slice(u * P, (u + 1) * P)
+            y_bank = psum.tile([P, O], F32, name=f"y_bank{u}")
+            nc.tensor.matmul_mx(
+                out=y_bank[:],
+                lhsT=wb_all[:, cols].bitcast(FP8X4), lhsT_scale=wb_plane[:, cols],
+                rhs=hid_codes[:].bitcast(FP8X4), rhs_scale=hid_plane[:],
+                start=True, stop=True,
+            )
+            y_rows = sb_tile([P, O], F32, f"y_rows{u}")
+            if u == 0:
+                nc.vector.tensor_copy(y_rows[:], y_bank[:])
+                nc.sync.dma_start(out[cols, :], y_rows[:])
+            else:
+                nc.scalar.copy(y_rows[:], y_bank[:])
+                nc.scalar.dma_start(out[cols, :], y_rows[:])

@@ -1,6 +1,7 @@
 from contextlib import ExitStack
 
 import concourse.mybir as mybir
+from concourse.masks import make_identity
 
 F32 = mybir.dt.float32
 BF16 = mybir.dt.bfloat16
@@ -15,9 +16,15 @@ MAX = mybir.AluOpType.max
 
 K, J, R, T, F, Z, M, O, C, N = 512, 256, 512, 1024, 1024, 512, 1024, 128, 512, 256
 P = 128
-PACK = 4
+SLOTS = 4
+LAST = SLOTS - 1
+QUADS = 4
+QUAD = P // QUADS
+SCALE_ROWS = 4
+PER_COLUMN = 16
 HALF = R // 2
-HM = HALF // PACK
+HALF_M = HALF // SLOTS
+PAIR = 2
 
 FLOPS = 2 * K * R * J + 2 * Z * R * J + 2 * R * N * O
 
@@ -31,17 +38,17 @@ def tile_picked_tokens_codegap_two_answered_one_plain_kernel(
         pool = ctx.enter_context(tc.tile_pool(name="sbuf", bufs=1))
         psum = ctx.enter_context(tc.psum_pool(name="psum", bufs=1))
 
-        def sb_tile(shape, dtype, name):
-            return pool.tile(shape, dtype, name=name, align_bytes=64)
+        def sb_tile(shape, dtype, name, tag=None):
+            return pool.tile(shape, dtype, name=name, tag=tag or name, align_bytes=64)
 
         def load_list(src, name):
             tile = sb_tile(list(src.shape), U16, name)
             nc.sync.dma_start(tile[:], src)
             return tile
 
-        def load_rows(src, name):
-            tile = sb_tile([P, PACK], F32, name)
-            nc.sync.dma_start(tile[:], src.rearrange("(p t) o -> p (t o)", t=PACK))
+        def load_factors(src, name):
+            tile = sb_tile([P, SLOTS], F32, name)
+            nc.sync.dma_start(tile[:], src.rearrange("(p s) o -> p (s o)", s=SLOTS))
             return tile
 
         def zeroed_plane(width, name):
@@ -49,176 +56,204 @@ def tile_picked_tokens_codegap_two_answered_one_plain_kernel(
             nc.vector.memset(tile[:].bitcast(I32), 0)
             return tile
 
-        def load_plane(tile, src):
-            for q in range(4):
+        def scale_rows(plane, q):
+            return plane[QUAD * q : QUAD * q + SCALE_ROWS, :].bitcast(I32)
+
+        def load_plane(plane, src):
+            for q in range(QUADS):
                 nc.sync.dma_start(
-                    tile[32 * q : 32 * q + 4, :].bitcast(I32), src[0, 4 * q : 4 * q + 4, :].bitcast(I32)
+                    scale_rows(plane, q), src[0, SCALE_ROWS * q : SCALE_ROWS * (q + 1), :].bitcast(I32)
                 )
 
-        xt_plane = zeroed_plane(T, "xt_plane")
         xo_plane = zeroed_plane(M, "xo_plane")
         w2_plane = zeroed_plane(R, "w2_plane")
-        wb_plane = zeroed_plane(N, "wb_plane")
+        xt_plane = zeroed_plane(T, "xt_plane")
         board = []
-        for t in range(PACK):
-            tile = sb_tile([P, C], F32, f"board{t}")
+        for s in range(SLOTS):
+            tile = sb_tile([P, C], F32, f"board{s}")
             nc.vector.memset(tile[:], 0.0)
             board.append(tile)
+        wb_plane = zeroed_plane(N, "wb_plane")
 
-        ua_rows = ua.rearrange("(p j) f -> p j f", j=PACK)
-        table = [sb_tile([P, F], F32, f"table{j}") for j in range(PACK)]
+        ua_rows = ua.rearrange("(p s) f -> p s f", s=SLOTS)
+        table = [sb_tile([P, F], F32, f"table{s}") for s in range(SLOTS)]
         xt_all = sb_tile([P, T], U16, "xt_all")
         xo_all = sb_tile([P, M], U16, "xo_all")
         w2_all = sb_tile([P, R], I32, "w2_all")
         list2 = load_list(offs2, "list2")
         nc.scalar.dma_start(table[0][:], ua_rows[:, 0, :])
-        ha_t = load_rows(ha, "ha_t")
+        ha_t = load_factors(ha, "ha_t")
         list3 = load_list(offs3, "list3")
-        hb_t = load_rows(hb, "hb_t")
+        hb_t = load_factors(hb, "hb_t")
+        xt_stage = sb_tile([SCALE_ROWS, QUADS, T // 4], I32, "xt_stage")
+        nc.scalar.dma_start(xt_stage[:], xt_scales[0].bitcast(I32).rearrange("(q i) w -> i q w", i=SCALE_ROWS))
         list1 = load_list(offs, "list1")
-        nc.scalar.dma_start(xt_all[:].bitcast(I32), xt_words[0].bitcast(I32))
         nc.scalar.dma_start(table[1][:], ua_rows[:, 1, :])
-        load_plane(xt_plane, xt_scales)
+        nc.sync.dma_start(xt_all[:].bitcast(I32), xt_words[0].bitcast(I32))
         list4 = load_list(offs4, "list4")
         nc.sync.dma_start(xo_all[:].bitcast(I32), xo_words[0].bitcast(I32))
-        nc.sync.dma_start(table[2][:], ua_rows[:, 2, :])
         load_plane(xo_plane, xo_scales)
-        nc.sync.dma_start(w2_all[:], w2_words[0].rearrange("p n t -> p (n t)").bitcast(I32))
-        load_plane(w2_plane, w2_scales)
+        nc.sync.dma_start(table[2][:], ua_rows[:, 2, :])
         nc.sync.dma_start(table[3][:], ua_rows[:, 3, :])
+        load_plane(w2_plane, w2_scales)
+        nc.sync.dma_start(w2_all[:], w2_words[0].rearrange("p n s -> p (n s)").bitcast(I32))
         list5 = load_list(offs5, "list5")
-        sa_t = load_rows(sa, "sa_t")
+        sa_t = load_factors(sa, "sa_t")
         list6 = load_list(offs6, "list6")
         list7 = load_list(offs7, "list7")
-        sb_t = load_rows(sb, "sb_t")
+        sb_t = load_factors(sb, "sb_t")
         wb_all = sb_tile([P, N], I32, "wb_all")
-        nc.sync.dma_start(wb_all[:], wb_words[0].rearrange("p n t -> p (n t)").bitcast(I32))
+        nc.sync.dma_start(wb_all[:], wb_words[0].rearrange("p n s -> p (n s)").bitcast(I32))
         load_plane(wb_plane, wb_scales)
 
-        first = [sb_tile([P, R], F32, f"first{j}") for j in range(PACK)]
-        second = [sb_tile([P, R], F32, f"second{j}") for j in range(PACK)]
-        diff = [sb_tile([P, PACK, PACK, HM], BF16, f"diff{h}") for h in range(2)]
-        grouped = [sb_tile([P, PACK, HM, PACK], BF16, f"grouped{h}") for h in range(2)]
-        wc_codes = [sb_tile([P, P], I32, f"wc_codes{t}") for t in range(PACK)]
-        wc_plane = [sb_tile([P, P], U8, f"wc_plane{t}") for t in range(PACK)]
+        first = [sb_tile([P, R], F32, f"first{ks}") for ks in range(SLOTS)]
+        second = [sb_tile([P, R], F32, f"second{ks}") for ks in range(SLOTS)]
+        diff = [sb_tile([P, LAST, HALF], BF16, f"diff{h}") for h in range(2)]
+        wc_codes = sb_tile([P, R], I32, "wc_codes")
+        wc_plane = sb_tile([P, R], U8, "wc_plane")
 
-        def fetch(j, lo, hi):
+        warm = sb_tile([P, 2], F32, "warm")
+        nc.gpsimd.memset(warm[:, 0:1], 0.0)
+        nc.scalar.activation(warm[:, 1:2], warm[:, 0:1], COPY)
+
+        def fetch(ks, lo, hi):
             for dst, lst, step in ((first, list2, ha_t), (second, list3, hb_t)):
                 nc.scalar.activation(
-                    dst[j][:, lo:hi], table[j][:].indirect(lst[:, lo // 16 : hi // 16]), COPY,
-                    scale=step[:, j : j + 1],
+                    dst[ks][:, lo:hi],
+                    table[ks][:].indirect(lst[:, lo // PER_COLUMN : hi // PER_COLUMN]),
+                    COPY,
+                    scale=step[:, ks : ks + 1],
                 )
 
-        def subtract(j, h):
+        def subtract(ks, h):
+            cols = slice(h * HALF, (h + 1) * HALF)
+            nc.vector.tensor_tensor(diff[h][:, ks, :], first[ks][:, cols], second[ks][:, cols], SUB)
+
+        def weave(h):
+            nc.vector.tensor_copy(
+                woven[:, :, h * HALF_M : (h + 1) * HALF_M, 0:LAST].rearrange("p rs (c i) ks -> p c rs i ks", i=PAIR),
+                diff[h][:].rearrange("p ks (c i rs) -> p c rs i ks", i=PAIR, rs=SLOTS),
+            )
+
+        def subtract_into_woven(h, rs0, rs1):
             cols = slice(h * HALF, (h + 1) * HALF)
             nc.vector.tensor_tensor(
-                diff[h][:, j, :, :].rearrange("p t m -> p m t"),
-                first[j][:, cols].rearrange("p (m t) -> p m t", t=PACK),
-                second[j][:, cols].rearrange("p (m t) -> p m t", t=PACK),
+                woven[:, rs0:rs1, h * HALF_M : (h + 1) * HALF_M, LAST].rearrange("p rs (c i) -> p c rs i", i=PAIR),
+                first[LAST][:, cols].rearrange("p (c i rs) -> p c rs i", i=PAIR, rs=SLOTS)[:, :, rs0:rs1, :],
+                second[LAST][:, cols].rearrange("p (c i rs) -> p c rs i", i=PAIR, rs=SLOTS)[:, :, rs0:rs1, :],
                 SUB,
             )
 
-        def weave(h, t0, t1):
-            nc.vector.tensor_copy(
-                grouped[h][:, t0:t1, :, :].rearrange("p t m j -> p (t m) j"),
-                diff[h][:, :, t0:t1, :].rearrange("p j t m -> p (t m) j"),
-            )
-
-        def quantise(h, t):
-            cols = slice(h * HM, (h + 1) * HM)
+        def quantise(rs0, rs1):
             nc.vector.quantize_mx(
-                out=wc_codes[t][:, cols].bitcast(FP8X4),
-                scales=wc_plane[t][:, cols],
-                in_=grouped[h][:, t, :, :].rearrange("p m j -> p (m j)"),
+                out=wc_codes[:, rs0 * P : rs1 * P].bitcast(FP8X4),
+                scales=wc_plane[:, rs0 * P : rs1 * P],
+                in_=woven[:, rs0:rs1, :, :].rearrange("p rs m ks -> p (rs m ks)"),
             )
 
-        def pick(words_all, plane_all, lst, name):
-            words = sb_tile([P, J], U16, name + "_words")
-            plane = sb_tile([P, J], U8, name + "_plane")
-            nc.vector.tensor_copy(words[:], words_all[:].indirect(lst[:]))
-            nc.vector.tensor_copy(plane[:], plane_all[:].indirect(lst[:]))
-            return words, plane
+        xt_pick = sb_tile([P, J], U16, "xt_pick")
+        xo_pick = sb_tile([P, J], U16, "xo_pick")
+        xt_pick_plane = sb_tile([P, J], U8, "xt_pick_plane")
+        xo_pick_plane = sb_tile([P, J], U8, "xo_pick_plane")
+        for q in range(QUADS):
+            nc.vector.tensor_copy(scale_rows(xt_plane, q), xt_stage[:, q, :])
+        nc.vector.tensor_copy(xt_pick_plane[:], xt_plane[:].indirect(list1[:]))
+        nc.vector.tensor_copy(xt_pick[:], xt_all[:].indirect(list1[:]))
+        nc.vector.tensor_copy(xo_pick[:], xo_all[:].indirect(list4[:]))
+        nc.vector.tensor_copy(xo_pick_plane[:], xo_plane[:].indirect(list4[:]))
 
-        xt_pick, xt_pick_plane = pick(xt_all, xt_plane, list1, "xt_pick")
-        fetch(0, 0, R)
-        subtract(0, 0)
-        subtract(0, 1)
-        xo_pick, xo_pick_plane = pick(xo_all, xo_plane, list4, "xo_pick")
-        fetch(1, 0, R)
-        subtract(1, 0)
-        subtract(1, 1)
-        w2_dealt = sb_tile([P, PACK, P], I32, "w2_dealt")
-        w2_dealt_plane = sb_tile([P, PACK, P], U8, "w2_dealt_plane")
-        nc.vector.tensor_copy(w2_dealt[:], w2_all[:].rearrange("p (m t) -> p t m", t=PACK))
-        nc.vector.tensor_copy(w2_dealt_plane[:], w2_plane[:].rearrange("p (m t) -> p t m", t=PACK))
-        b_bank = [psum.tile([P, 2, J], F32, name=f"b_bank{u}") for u in range(2)]
-        for t in range(PACK):
-            nc.tensor.matmul_mx(
-                out=b_bank[t // 2][:, t % 2, :],
-                lhsT=w2_dealt[:, t, :].bitcast(FP8X4), lhsT_scale=w2_dealt_plane[:, t, :],
-                rhs=xo_pick[:].bitcast(FP4X4), rhs_scale=xo_pick_plane[:],
-                start=True, stop=True,
-            )
+        woven = sb_tile([P, SLOTS, P, SLOTS], BF16, "woven")
+        for ks in range(LAST - 1):
+            fetch(ks, 0, R)
+            for h in range(2):
+                subtract(ks, h)
+        for h in range(2):
+            fetch(LAST - 1, h * HALF, (h + 1) * HALF)
+            subtract(LAST - 1, h)
+            weave(h)
+        fetch(LAST, 0, HALF)
+        subtract_into_woven(0, 0, SLOTS)
+        fetch(LAST, HALF, R)
+        subtract_into_woven(1, 0, 1)
+        rest = sb_tile([P, HALF_M, LAST], BF16, "rest")
+        nc.vector.tensor_tensor(
+            rest[:],
+            first[LAST][:, HALF:].rearrange("p (m rs) -> p m rs", rs=SLOTS)[:, :, 1:],
+            second[LAST][:, HALF:].rearrange("p (m rs) -> p m rs", rs=SLOTS)[:, :, 1:],
+            SUB,
+        )
+        quantise(0, 1)
+        nc.vector.tensor_copy(
+            woven[:, 1:, HALF_M:, LAST].rearrange("p rs (c i) -> p c rs i", i=PAIR),
+            rest[:].rearrange("p (c i) rs -> p c rs i", i=PAIR),
+        )
+        quantise(1, SLOTS)
 
-        fetch(2, 0, HALF)
-        subtract(2, 0)
-        fetch(3, 0, HALF)
-        subtract(3, 0)
-        fetch(2, HALF, R)
-        weave(0, 0, PACK)
-        subtract(2, 1)
-        for t in range(PACK):
-            quantise(0, t)
-        fetch(3, HALF, R)
-        subtract(3, 1)
-        weave(1, 0, 1)
-        weave(1, 1, 2)
-        quantise(1, 0)
-        weave(1, 2, 4)
-        for t in range(1, PACK):
-            quantise(1, t)
-
-        hid_rows = sb_tile([P, PACK, O], BF16, "hid_rows")
-        for t in range(PACK):
-            a_bank = psum.tile([P, J], F32, name=f"a_bank{t}")
+        a_rows = []
+        for s in range(SLOTS):
+            a_bank = psum.tile([P, J], F32, name=f"a_bank{s}")
             nc.tensor.matmul_mx(
                 out=a_bank[:],
-                lhsT=wc_codes[t][:].bitcast(FP8X4), lhsT_scale=wc_plane[t][:],
+                lhsT=wc_codes[:, s * P : (s + 1) * P].bitcast(FP8X4), lhsT_scale=wc_plane[:, s * P : (s + 1) * P],
                 rhs=xt_pick[:].bitcast(FP4X4), rhs_scale=xt_pick_plane[:],
                 start=True, stop=True,
             )
-            a_rows = sb_tile([P, J], F32, f"a_rows{t}")
-            nc.scalar.copy(a_rows[:], a_bank[:])
-            nc.vector.tensor_copy(board[t][:].indirect(list5[:]), a_rows[:])
-            read = sb_tile([P, J], F32, f"read{t}")
-            nc.scalar.activation(read[:], board[t][:].indirect(list6[:]), COPY, scale=sa_t[:, t : t + 1])
-            answer = sb_tile([P, J], F32, f"answer{t}")
-            nc.vector.tensor_tensor(answer[:], b_bank[t // 2][:, t % 2, :], read[:], MAX)
+            rows = sb_tile([P, J], F32, f"a_rows{s}")
+            nc.scalar.copy(rows[:], a_bank[:])
+            a_rows.append(rows)
+
+        identity = sb_tile([P, P], F32, "identity")
+        make_identity(nc, identity[:])
+        bt_rows = sb_tile([P, J // P, SLOTS, P], F32, "bt_rows", tag="wc_codes")
+        for u in range(J // P):
+            cols = slice(u * P, (u + 1) * P)
+            bt_bank = psum.tile([P, R], F32, name=f"bt_bank{u}", tag=f"side{u}")
+            nc.tensor.matmul_mx(
+                out=bt_bank[:],
+                lhsT=xo_pick[:, cols].bitcast(FP4X4), lhsT_scale=xo_pick_plane[:, cols],
+                rhs=w2_all[:].bitcast(FP8X4), rhs_scale=w2_plane[:],
+                start=True, stop=True,
+            )
+            nc.scalar.copy(bt_rows[:, u, :, :], bt_bank[:].rearrange("p (m s) -> p s m", s=SLOTS))
+        b_bank = [psum.tile([P, 2, J], F32, name=f"b_bank{v}") for v in range(SLOTS // 2)]
+        for s in range(SLOTS):
+            for u in range(J // P):
+                nc.tensor.transpose(b_bank[s // 2][:, s % 2, u * P : (u + 1) * P], bt_rows[:, u, s, :], identity[:])
+
+        for s in range(SLOTS):
+            nc.vector.tensor_copy(board[s][:].indirect(list5[:]), a_rows[s][:])
+        read = [sb_tile([P, J], F32, f"read{s}") for s in range(SLOTS)]
+        for s in range(SLOTS):
+            nc.scalar.activation(read[s][:], board[s][:].indirect(list6[:]), COPY, scale=sa_t[:, s : s + 1])
+        answer = [sb_tile([P, J], F32, f"answer{s}") for s in range(SLOTS)]
+        for s in range(SLOTS):
+            nc.vector.tensor_tensor(answer[s][:], b_bank[s // 2][:, s % 2, :], read[s][:], MAX)
+        hid_rows = sb_tile([P, SLOTS, O], BF16, "hid_rows")
+        for s in range(SLOTS):
             nc.scalar.activation(
-                hid_rows[:, t, :], answer[:].indirect(list7[:]), COPY, scale=sb_t[:, t : t + 1]
+                hid_rows[:, s, :], answer[s][:].indirect(list7[:]), COPY, scale=sb_t[:, s : s + 1]
             )
 
-        hid_grouped = sb_tile([P, O, PACK], BF16, "hid_grouped")
-        nc.vector.tensor_copy(hid_grouped[:], hid_rows[:].rearrange("p t o -> p o t"))
+        hid_woven = sb_tile([P, O, SLOTS], BF16, "hid_woven")
+        nc.vector.tensor_copy(hid_woven[:, :, 0:LAST], hid_rows[:, 0:LAST, :].rearrange("p s o -> p o s"))
+        nc.vector.tensor_copy(hid_woven[:, :, LAST], hid_rows[:, LAST, :])
         hid_codes = sb_tile([P, O], I32, "hid_codes")
         hid_plane = sb_tile([P, O], U8, "hid_plane")
         nc.vector.quantize_mx(
             out=hid_codes[:].bitcast(FP8X4), scales=hid_plane[:],
-            in_=hid_grouped[:].rearrange("p o t -> p (o t)"),
+            in_=hid_woven[:].rearrange("p o s -> p (o s)"),
         )
-        for u in range(2):
-            cols = slice(u * P, (u + 1) * P)
-            y_bank = psum.tile([P, O], F32, name=f"y_bank{u}")
+
+        ways_out = ((nc.vector.tensor_copy, nc.sync), (nc.scalar.copy, nc.scalar))
+        for u, (empty, queue) in enumerate(ways_out):
+            block = slice(u * P, (u + 1) * P)
+            y_bank = psum.tile([P, O], F32, name=f"y_bank{u}", tag=f"side{u}")
             nc.tensor.matmul_mx(
                 out=y_bank[:],
-                lhsT=wb_all[:, cols].bitcast(FP8X4), lhsT_scale=wb_plane[:, cols],
+                lhsT=wb_all[:, block].bitcast(FP8X4), lhsT_scale=wb_plane[:, block],
                 rhs=hid_codes[:].bitcast(FP8X4), rhs_scale=hid_plane[:],
                 start=True, stop=True,
             )
             y_rows = sb_tile([P, O], F32, f"y_rows{u}")
-            if u == 0:
-                nc.vector.tensor_copy(y_rows[:], y_bank[:])
-                nc.sync.dma_start(out[cols, :], y_rows[:])
-            else:
-                nc.scalar.copy(y_rows[:], y_bank[:])
-                nc.scalar.dma_start(out[cols, :], y_rows[:])
+            empty(y_rows[:], y_bank[:])
+            queue.dma_start(out[block, :], y_rows[:])

from contextlib import ExitStack

import concourse.mybir as mybir
from concourse.masks import make_identity

F32 = mybir.dt.float32
BF16 = mybir.dt.bfloat16
I32 = mybir.dt.int32
U16 = mybir.dt.uint16
U8 = mybir.dt.uint8
FP8X4 = mybir.dt.float8_e4m3fn_x4
FP4X4 = mybir.dt.float4_e2m1fn_x4
COPY = mybir.ActivationFunctionType.Copy
SUB = mybir.AluOpType.subtract
MAX = mybir.AluOpType.max

K, J, R, T, F, Z, M, O, C, N = 512, 256, 512, 1024, 1024, 512, 1024, 128, 512, 256
P = 128
SLOTS = 4
LAST = SLOTS - 1
QUADS = 4
QUAD = P // QUADS
SCALE_ROWS = 4
PER_COLUMN = 16
HALF = R // 2
HALF_M = HALF // SLOTS
PAIR = 2

FLOPS = 2 * K * R * J + 2 * Z * R * J + 2 * R * N * O


def tile_picked_tokens_codegap_two_answered_one_plain_kernel(
    tc, xt_words, xt_scales, ua, ha, hb, xo_words, xo_scales, w2_words, w2_scales, sa, sb,
    wb_words, wb_scales, offs, offs2, offs3, offs4, offs5, offs6, offs7, out,
):
    nc = tc.nc
    with ExitStack() as ctx:
        pool = ctx.enter_context(tc.tile_pool(name="sbuf", bufs=1))
        psum = ctx.enter_context(tc.psum_pool(name="psum", bufs=1))

        def sb_tile(shape, dtype, name, tag=None):
            return pool.tile(shape, dtype, name=name, tag=tag or name, align_bytes=64)

        def load_list(src, name):
            tile = sb_tile(list(src.shape), U16, name)
            nc.sync.dma_start(tile[:], src)
            return tile

        def load_factors(src, name):
            tile = sb_tile([P, SLOTS], F32, name)
            nc.sync.dma_start(tile[:], src.rearrange("(p s) o -> p (s o)", s=SLOTS))
            return tile

        def zeroed_plane(width, name):
            tile = sb_tile([P, width], U8, name)
            nc.vector.memset(tile[:].bitcast(I32), 0)
            return tile

        def scale_rows(plane, q):
            return plane[QUAD * q : QUAD * q + SCALE_ROWS, :].bitcast(I32)

        def load_plane(plane, src):
            for q in range(QUADS):
                nc.sync.dma_start(
                    scale_rows(plane, q), src[0, SCALE_ROWS * q : SCALE_ROWS * (q + 1), :].bitcast(I32)
                )

        xo_plane = zeroed_plane(M, "xo_plane")
        w2_plane = zeroed_plane(R, "w2_plane")
        xt_plane = zeroed_plane(T, "xt_plane")
        board = []
        for s in range(SLOTS):
            tile = sb_tile([P, C], F32, f"board{s}")
            nc.vector.memset(tile[:], 0.0)
            board.append(tile)
        wb_plane = zeroed_plane(N, "wb_plane")

        ua_rows = ua.rearrange("(p s) f -> p s f", s=SLOTS)
        table = [sb_tile([P, F], F32, f"table{s}") for s in range(SLOTS)]
        xt_all = sb_tile([P, T], U16, "xt_all")
        xo_all = sb_tile([P, M], U16, "xo_all")
        w2_all = sb_tile([P, R], I32, "w2_all")
        list2 = load_list(offs2, "list2")
        nc.scalar.dma_start(table[0][:], ua_rows[:, 0, :])
        ha_t = load_factors(ha, "ha_t")
        list3 = load_list(offs3, "list3")
        hb_t = load_factors(hb, "hb_t")
        xt_stage = sb_tile([SCALE_ROWS, QUADS, T // 4], I32, "xt_stage")
        nc.scalar.dma_start(xt_stage[:], xt_scales[0].bitcast(I32).rearrange("(q i) w -> i q w", i=SCALE_ROWS))
        list1 = load_list(offs, "list1")
        nc.scalar.dma_start(table[1][:], ua_rows[:, 1, :])
        nc.sync.dma_start(xt_all[:].bitcast(I32), xt_words[0].bitcast(I32))
        list4 = load_list(offs4, "list4")
        nc.sync.dma_start(xo_all[:].bitcast(I32), xo_words[0].bitcast(I32))
        load_plane(xo_plane, xo_scales)
        nc.sync.dma_start(table[2][:], ua_rows[:, 2, :])
        nc.sync.dma_start(table[3][:], ua_rows[:, 3, :])
        load_plane(w2_plane, w2_scales)
        nc.sync.dma_start(w2_all[:], w2_words[0].rearrange("p n s -> p (n s)").bitcast(I32))
        list5 = load_list(offs5, "list5")
        sa_t = load_factors(sa, "sa_t")
        list6 = load_list(offs6, "list6")
        list7 = load_list(offs7, "list7")
        sb_t = load_factors(sb, "sb_t")
        wb_all = sb_tile([P, N], I32, "wb_all")
        nc.sync.dma_start(wb_all[:], wb_words[0].rearrange("p n s -> p (n s)").bitcast(I32))
        load_plane(wb_plane, wb_scales)

        first = [sb_tile([P, R], F32, f"first{ks}") for ks in range(SLOTS)]
        second = [sb_tile([P, R], F32, f"second{ks}") for ks in range(SLOTS)]
        diff = [sb_tile([P, LAST, HALF], BF16, f"diff{h}") for h in range(2)]
        wc_codes = sb_tile([P, R], I32, "wc_codes")
        wc_plane = sb_tile([P, R], U8, "wc_plane")

        warm = sb_tile([P, 2], F32, "warm")
        nc.gpsimd.memset(warm[:, 0:1], 0.0)
        nc.scalar.activation(warm[:, 1:2], warm[:, 0:1], COPY)

        def fetch(ks, lo, hi):
            for dst, lst, step in ((first, list2, ha_t), (second, list3, hb_t)):
                nc.scalar.activation(
                    dst[ks][:, lo:hi],
                    table[ks][:].indirect(lst[:, lo // PER_COLUMN : hi // PER_COLUMN]),
                    COPY,
                    scale=step[:, ks : ks + 1],
                )

        def subtract(ks, h):
            cols = slice(h * HALF, (h + 1) * HALF)
            nc.vector.tensor_tensor(diff[h][:, ks, :], first[ks][:, cols], second[ks][:, cols], SUB)

        def weave(h):
            nc.vector.tensor_copy(
                woven[:, :, h * HALF_M : (h + 1) * HALF_M, 0:LAST].rearrange("p rs (c i) ks -> p c rs i ks", i=PAIR),
                diff[h][:].rearrange("p ks (c i rs) -> p c rs i ks", i=PAIR, rs=SLOTS),
            )

        def subtract_into_woven(h, rs0, rs1):
            cols = slice(h * HALF, (h + 1) * HALF)
            nc.vector.tensor_tensor(
                woven[:, rs0:rs1, h * HALF_M : (h + 1) * HALF_M, LAST].rearrange("p rs (c i) -> p c rs i", i=PAIR),
                first[LAST][:, cols].rearrange("p (c i rs) -> p c rs i", i=PAIR, rs=SLOTS)[:, :, rs0:rs1, :],
                second[LAST][:, cols].rearrange("p (c i rs) -> p c rs i", i=PAIR, rs=SLOTS)[:, :, rs0:rs1, :],
                SUB,
            )

        def quantise(rs0, rs1):
            nc.vector.quantize_mx(
                out=wc_codes[:, rs0 * P : rs1 * P].bitcast(FP8X4),
                scales=wc_plane[:, rs0 * P : rs1 * P],
                in_=woven[:, rs0:rs1, :, :].rearrange("p rs m ks -> p (rs m ks)"),
            )

        xt_pick = sb_tile([P, J], U16, "xt_pick")
        xo_pick = sb_tile([P, J], U16, "xo_pick")
        xt_pick_plane = sb_tile([P, J], U8, "xt_pick_plane")
        xo_pick_plane = sb_tile([P, J], U8, "xo_pick_plane")
        for q in range(QUADS):
            nc.vector.tensor_copy(scale_rows(xt_plane, q), xt_stage[:, q, :])
        nc.vector.tensor_copy(xt_pick_plane[:], xt_plane[:].indirect(list1[:]))
        nc.vector.tensor_copy(xt_pick[:], xt_all[:].indirect(list1[:]))
        nc.vector.tensor_copy(xo_pick[:], xo_all[:].indirect(list4[:]))
        nc.vector.tensor_copy(xo_pick_plane[:], xo_plane[:].indirect(list4[:]))

        woven = sb_tile([P, SLOTS, P, SLOTS], BF16, "woven")
        for ks in range(LAST - 1):
            fetch(ks, 0, R)
            for h in range(2):
                subtract(ks, h)
        for h in range(2):
            fetch(LAST - 1, h * HALF, (h + 1) * HALF)
            subtract(LAST - 1, h)
            weave(h)
        fetch(LAST, 0, HALF)
        subtract_into_woven(0, 0, SLOTS)
        fetch(LAST, HALF, R)
        subtract_into_woven(1, 0, 1)
        rest = sb_tile([P, HALF_M, LAST], BF16, "rest")
        nc.vector.tensor_tensor(
            rest[:],
            first[LAST][:, HALF:].rearrange("p (m rs) -> p m rs", rs=SLOTS)[:, :, 1:],
            second[LAST][:, HALF:].rearrange("p (m rs) -> p m rs", rs=SLOTS)[:, :, 1:],
            SUB,
        )
        quantise(0, 1)
        nc.vector.tensor_copy(
            woven[:, 1:, HALF_M:, LAST].rearrange("p rs (c i) -> p c rs i", i=PAIR),
            rest[:].rearrange("p (c i) rs -> p c rs i", i=PAIR),
        )
        quantise(1, SLOTS)

        a_rows = []
        for s in range(SLOTS):
            a_bank = psum.tile([P, J], F32, name=f"a_bank{s}")
            nc.tensor.matmul_mx(
                out=a_bank[:],
                lhsT=wc_codes[:, s * P : (s + 1) * P].bitcast(FP8X4), lhsT_scale=wc_plane[:, s * P : (s + 1) * P],
                rhs=xt_pick[:].bitcast(FP4X4), rhs_scale=xt_pick_plane[:],
                start=True, stop=True,
            )
            rows = sb_tile([P, J], F32, f"a_rows{s}")
            nc.scalar.copy(rows[:], a_bank[:])
            a_rows.append(rows)

        identity = sb_tile([P, P], F32, "identity")
        make_identity(nc, identity[:])
        bt_rows = sb_tile([P, J // P, SLOTS, P], F32, "bt_rows", tag="wc_codes")
        for u in range(J // P):
            cols = slice(u * P, (u + 1) * P)
            bt_bank = psum.tile([P, R], F32, name=f"bt_bank{u}", tag=f"side{u}")
            nc.tensor.matmul_mx(
                out=bt_bank[:],
                lhsT=xo_pick[:, cols].bitcast(FP4X4), lhsT_scale=xo_pick_plane[:, cols],
                rhs=w2_all[:].bitcast(FP8X4), rhs_scale=w2_plane[:],
                start=True, stop=True,
            )
            nc.scalar.copy(bt_rows[:, u, :, :], bt_bank[:].rearrange("p (m s) -> p s m", s=SLOTS))
        b_bank = [psum.tile([P, 2, J], F32, name=f"b_bank{v}") for v in range(SLOTS // 2)]
        for s in range(SLOTS):
            for u in range(J // P):
                nc.tensor.transpose(b_bank[s // 2][:, s % 2, u * P : (u + 1) * P], bt_rows[:, u, s, :], identity[:])

        for s in range(SLOTS):
            nc.vector.tensor_copy(board[s][:].indirect(list5[:]), a_rows[s][:])
        read = [sb_tile([P, J], F32, f"read{s}") for s in range(SLOTS)]
        for s in range(SLOTS):
            nc.scalar.activation(read[s][:], board[s][:].indirect(list6[:]), COPY, scale=sa_t[:, s : s + 1])
        answer = [sb_tile([P, J], F32, f"answer{s}") for s in range(SLOTS)]
        for s in range(SLOTS):
            nc.vector.tensor_tensor(answer[s][:], b_bank[s // 2][:, s % 2, :], read[s][:], MAX)
        hid_rows = sb_tile([P, SLOTS, O], BF16, "hid_rows")
        for s in range(SLOTS):
            nc.scalar.activation(
                hid_rows[:, s, :], answer[s][:].indirect(list7[:]), COPY, scale=sb_t[:, s : s + 1]
            )

        hid_woven = sb_tile([P, O, SLOTS], BF16, "hid_woven")
        nc.vector.tensor_copy(hid_woven[:, :, 0:LAST], hid_rows[:, 0:LAST, :].rearrange("p s o -> p o s"))
        nc.vector.tensor_copy(hid_woven[:, :, LAST], hid_rows[:, LAST, :])
        hid_codes = sb_tile([P, O], I32, "hid_codes")
        hid_plane = sb_tile([P, O], U8, "hid_plane")
        nc.vector.quantize_mx(
            out=hid_codes[:].bitcast(FP8X4), scales=hid_plane[:],
            in_=hid_woven[:].rearrange("p o s -> p (o s)"),
        )

        ways_out = ((nc.vector.tensor_copy, nc.sync), (nc.scalar.copy, nc.scalar))
        for u, (empty, queue) in enumerate(ways_out):
            block = slice(u * P, (u + 1) * P)
            y_bank = psum.tile([P, O], F32, name=f"y_bank{u}", tag=f"side{u}")
            nc.tensor.matmul_mx(
                out=y_bank[:],
                lhsT=wb_all[:, block].bitcast(FP8X4), lhsT_scale=wb_plane[:, block],
                rhs=hid_codes[:].bitcast(FP8X4), rhs_scale=hid_plane[:],
                start=True, stop=True,
            )
            y_rows = sb_tile([P, O], F32, f"y_rows{u}")
            empty(y_rows[:], y_bank[:])
            queue.dma_start(out[block, :], y_rows[:])
